import numpy as np
import ml_dtypes


def mxq(x, axis, fmt="e4m3"):
    dtype, down = {"e4m3": (ml_dtypes.float8_e4m3fn, 7), "e5m2": (ml_dtypes.float8_e5m2, 14)}[fmt]
    v = np.moveaxis(np.asarray(x, np.float32).astype(ml_dtypes.bfloat16).astype(np.float64), axis, -1)
    blocks = v.reshape(v.shape[:-1] + (-1, 32))
    amax = np.abs(blocks).max(-1, keepdims=True)
    byte = np.maximum(np.where(amax > 0, np.frexp(amax)[1] - 1 + 127, 0) - down, 1)
    scale = np.exp2(byte - 127.0)
    codes = (blocks / scale).astype(np.float32).astype(dtype).astype(np.float64)
    return np.moveaxis((codes * scale).reshape(v.shape), -1, axis)


WIDE = False


def mx_kscale(k):
    if not WIDE:
        return np.ones(k)
    levels = np.array([10, -10, 5, -5, 0])
    if k % 512:
        return np.exp2(np.random.permutation(np.resize(levels, k // 32))).repeat(32)
    a = np.empty((k // 512, 16))
    for p in range(k // 512):
        a[p, :8] = np.random.permutation(np.resize(levels, 8))
        for g in range(8):
            far = levels[np.abs(levels - a[p, g]) >= 10]
            a[p, g + 8] = far[np.random.randint(len(far))]
    return np.exp2(a.ravel()).repeat(32)


def f64(x):
    return np.asarray(x).astype(np.float64)


def striped(idx):
    return np.tile(idx.reshape(-1, 16).T, (8, 1)).astype(np.uint16)


def unstriped(offs):
    return offs[:16].T.reshape(-1).astype(np.int64)


def striped8(idx):
    return np.concatenate([x.reshape(-1, 16).T for x in idx]).astype(np.uint16)


def runs(offs, k):
    lists = np.stack([offs[16 * r : 16 * r + 16].T.reshape(-1) for r in range(8)]).astype(np.int64)
    return lists[np.arange(k) % 512 // 64]


def pack_weight(w):
    k, n = w.shape
    w = f64(np.asarray(w, np.float32).astype(ml_dtypes.bfloat16)).reshape(k // 32, 32, n)
    amax = np.abs(w).max(1)
    byte = np.clip(np.where(amax > 0, np.frexp(amax)[1] - 1 + 127 - 7, 1), 1, 254)
    scaled = (w * np.exp2(127.0 - byte)[:, None, :]).reshape(k, n).astype(np.float32)
    words = np.ascontiguousarray(scaled.reshape(k // 512, 128, 4, n).transpose(0, 1, 3, 2)).astype(ml_dtypes.float8_e4m3fn).view(np.uint8)
    return words, np.ascontiguousarray(byte.astype(np.uint8).reshape(k // 512, 16, n))


def unpack_weight(words, scales):
    g, p, n, _ = words.shape
    vals = np.ascontiguousarray(words).view(ml_dtypes.float8_e4m3fn).astype(np.float64) * np.repeat(np.exp2(scales.astype(np.float64) - 127.0), 8, axis=1)[..., None]
    return vals.transpose(0, 1, 3, 2).reshape(g * 512, n)

def planes(y):
    n, m = y.shape
    v = y.astype(np.float32).astype(ml_dtypes.bfloat16).astype(np.float64).reshape(n // 32, 32, m)
    top = np.abs(v).max(1)
    byte = np.clip(np.where(top > 0, np.frexp(top)[1] - 1 + 127 - 7, 1), 1, 254)
    codes = (v * np.exp2(127.0 - byte)[:, None, :]).reshape(n, m).astype(np.float32).astype(ml_dtypes.float8_e4m3fn).view(np.uint8)
    words = codes.reshape(n // 512, 128, 4, m).transpose(0, 1, 3, 2)
    return np.ascontiguousarray(words), np.ascontiguousarray(byte.astype(np.uint8).reshape(n // 512, 16, m))


K, T, S, N, G, H = 512, 2048, 512, 512, 2048, 512


def setup_inputs():
    n = np.random.standard_normal
    s = mx_kscale(K)[:, None]
    u = mx_kscale(S)
    packed_xT = pack_weight(n((K, T)) * s)
    packed_dT = pack_weight(n((K, G)) / s)
    return {
        "x_words": packed_xT[0],
        "x_scales": packed_xT[1],
        "d_words": packed_dT[0],
        "d_scales": packed_dT[1],
        "wv": (n((K, N)) / np.sqrt(K) / s).astype(np.float32),
        "gi": (np.random.uniform(0.5, 1.5, (H, 1)) / u[:, None]).astype(np.float32),
        "gt": (np.random.uniform(0.5, 1.5, (H, 1)) * u[:, None]).astype(np.float32),
        "offs": striped(np.random.permutation(T)[:S]),
        "kidx": striped8(np.random.randint(0, G, (8, H))),
        "vidx": striped(np.random.permutation(T)[:H]),
    }


def reference(x_words, x_scales, d_words, d_scales, wv, gi, gt, offs, kidx, vidx):
    x_vidx = unpack_weight(x_words, x_scales)[:, unstriped(vidx)]
    val = x_vidx.T @ mxq(f64(wv), 0, "e4m3")
    z = f64(gi) * val
    d_kidx = unpack_weight(d_words, d_scales)[np.arange(K)[:, None], runs(kidx, K)]
    xq = unpack_weight(x_words, x_scales)[:, unstriped(offs)]
    s = 0.0625 * (d_kidx.T @ xq)
    z2 = f64(gt) * np.tanh(s)
    out_0 = 0.0625 * ((mxq(z, 0, "e4m3").T @ mxq(z2, 0, "e4m3")))
    return (out_0,) + planes(out_0)

@@ -1,0 +1,204 @@
+from contextlib import ExitStack
+
+import concourse.mybir as mybir
+from concourse.masks import make_identity
+
+K, T, S, N, G, H = 512, 2048, 512, 512, 2048, 512
+FLOPS = 3 * 2 * 512 * 512 * 512
+
+F32 = mybir.dt.float32
+BF16 = mybir.dt.bfloat16
+U32 = mybir.dt.uint32
+I32 = mybir.dt.int32
+U16 = mybir.dt.uint16
+U8 = mybir.dt.uint8
+FP8X4 = mybir.dt.float8_e4m3fn_x4
+ACT = mybir.ActivationFunctionType
+MULT = mybir.AluOpType.mult
+
+P = 128
+PACK = 4
+CHUNK = 128
+CHUNKS = S // CHUNK
+HALF = N // 2
+
+
+def tile_picked_listpq_tanh_po_kernel(
+    tc, x_words, x_scales, d_words, d_scales, wv, gi, gt, offs, kidx, vidx, out_0, out_1, out_2
+):
+    nc = tc.nc
+    with ExitStack() as ctx:
+        sb = ctx.enter_context(tc.tile_pool(name="sb", bufs=1))
+        ps = ctx.enter_context(tc.psum_pool(name="ps", bufs=1))
+
+        def tile(shape, dtype, name):
+            return sb.tile(shape, dtype, name=name, align_bytes=64)
+
+        def mx(out, lhs_words, lhs_scales, rhs_words, rhs_scales):
+            nc.tensor.matmul_mx(
+                out=out, lhsT=lhs_words.bitcast(FP8X4), lhsT_scale=lhs_scales,
+                rhs=rhs_words.bitcast(FP8X4), rhs_scale=rhs_scales, start=True, stop=True,
+            )
+
+        def interleave_views(dst, src):
+            return (dst.rearrange("p (c i) t -> p c t i", i=4), src.rearrange("p t (c i) -> p c t i", i=4))
+
+        def deal_scales(dst, src):
+            nc.vector.tensor_copy(
+                out=dst[:].bitcast(I32).rearrange("p (t q w) -> p q t w", t=4, w=2),
+                in_=src[:].bitcast(I32).rearrange("p (q t w) -> p q t w", t=4, w=2),
+            )
+
+        vidx_t = sb.tile([P, H // 16], U16, name="vidx_t")
+        offs_t = sb.tile([P, S // 16], U16, name="offs_t")
+        kidx_t = sb.tile([P, H // 16], U16, name="kidx_t")
+        ds_win = tile([P, G], U8, "ds_win")
+        nc.sync.dma_start(vidx_t[:], vidx)
+        nc.sync.dma_start(offs_t[:], offs)
+        xs_win = tile([P, T], U8, "xs_win")
+        for q in range(4):
+            rows = x_scales[0, 4 * q : 4 * q + 4, :].bitcast(I32)
+            nc.sync.dma_start(
+                out=xs_win[32 * q : 32 * q + 32, :].bitcast(I32),
+                in_=rows.unsqueeze(0).to_broadcast([8, 4, T // 4]),
+            )
+        ident = tile([P, P], F32, "ident")
+        wv_raw = tile([P, PACK, N], F32, "wv_raw")
+        xw_win = tile([P, T], U32, "xw_win")
+        dw_win = tile([P, G], U32, "dw_win")
+        nc.sync.dma_start(out=wv_raw[:], in_=wv.rearrange("(p j) c -> p j c", j=PACK))
+        nc.sync.dma_start(out=xw_win[:].bitcast(I32), in_=x_words[0].rearrange("p n t -> p (n t)").bitcast(I32))
+        nc.sync.dma_start(kidx_t[:], kidx)
+        nc.sync.dma_start(out=dw_win[:].bitcast(I32), in_=d_words[0].rearrange("p n t -> p (n t)").bitcast(I32))
+        nc.vector.memset(ds_win[:].bitcast(I32), 0)
+        nc.gpsimd.dma_start(out=ds_win[0:P:8, :].bitcast(I32), in_=d_scales[0].bitcast(I32))
+
+        g_rows = tile([P, P], F32, "g_rows")
+        nc.gpsimd.memset(g_rows[:], 0.0)
+        for r, vec in enumerate((gi, gt)):
+            nc.gpsimd.dma_start(
+                out=g_rows[4 * r : 4 * r + 4, :].rearrange("t (q r) -> t q r", r=8),
+                in_=vec.rearrange("(q t r) o -> t q (r o)", t=4, r=8),
+            )
+        make_identity(nc, ident[:])
+        g_ps = ps.tile([P, P], F32, name="g_ps", tag="s3")
+        nc.tensor.transpose(g_ps[:], g_rows[:], ident[:])
+        g_cols = tile([P, 8], F32, "g_cols")
+        nc.scalar.copy(out=g_cols[:], in_=g_ps[:, 0:8])
+
+        xv_s_raw = tile([P, H], U8, "xv_s_raw")
+        xv_s = tile([P, H], U8, "xv_s")
+        xq_s = tile([P, S], U8, "xq_s")
+        dk_s_raw = tile([P, H], U8, "dk_s_raw")
+        dk_s = tile([P, H], U8, "dk_s")
+        dk_plane = tile([P, H], U8, "dk_plane")
+        nc.vector.memset(dk_plane[:].bitcast(I32), 0)
+        nc.vector.tensor_copy(xv_s_raw[:], xs_win[:].indirect(vidx_t[:]))
+        nc.vector.tensor_copy(xq_s[:], xs_win[:].indirect(offs_t[:]))
+        deal_scales(xv_s, xv_s_raw)
+
+        wv_bf = tile([P, N, PACK], BF16, "wv_bf")
+        wv_w = tile([P, N], U32, "wv_w")
+        wv_s = tile([P, N], U8, "wv_s")
+        dst, src = interleave_views(wv_bf[:], wv_raw[:])
+        nc.scalar.copy(out=dst, in_=src)
+
+        xv_w = tile([P, H], U32, "xv_w")
+        xq_w = tile([P, S], U32, "xq_w")
+        dk_w_raw = tile([P, H], U32, "dk_w_raw")
+        dk_w = tile([P, H], U32, "dk_w")
+        nc.vector.tensor_copy(xv_w[:].rearrange("p (t q r) -> p q t r", t=4, r=8), xw_win[:].indirect(vidx_t[:]))
+        nc.vector.quantize_mx(out=wv_w[:].bitcast(FP8X4), scales=wv_s[:], in_=wv_bf[:].rearrange("p c t -> p (c t)"))
+        nc.vector.tensor_copy(dk_s_raw[:], ds_win[:].indirect(kidx_t[:]))
+        deal_scales(dk_s, dk_s_raw)
+        for j in range(4):
+            nc.sync.dma_start(out=dk_plane[j:P:32, :].bitcast(I32), in_=dk_s[8 * j : P : 32, :].bitcast(I32))
+        nc.vector.tensor_copy(xq_w[:], xw_win[:].indirect(offs_t[:]))
+        nc.vector.tensor_copy(dk_w_raw[:], dw_win[:].indirect(kidx_t[:]))
+        nc.vector.tensor_copy(
+            out=dk_w[:].rearrange("p (t q r) -> p q t r", t=4, r=8),
+            in_=dk_w_raw[:].rearrange("p (q t r) -> p q t r", t=4, r=8),
+        )
+
+        z_planes = tile([P, PACK, N], BF16, "z_planes")
+        for t in range(PACK):
+            keys = slice(t * P, (t + 1) * P)
+            val = ps.tile([P, N], F32, name="val%d" % t, tag="v%d" % t)
+            mx(val[:], xv_w[:, keys], xv_s[:, keys], wv_w[:], wv_s[:])
+            nc.scalar.activation(
+                out=z_planes[:, t, :].rearrange("p (u m) -> p u m", u=PACK),
+                in_=val[:].rearrange("p (m u) -> p u m", u=PACK),
+                func=ACT.Copy, scale=g_cols[:, t : t + 1],
+            )
+        z_bf = tile([P, N, PACK], BF16, "z_bf")
+        z_w = tile([P, N], U32, "z_w")
+        z_s = tile([P, N], U8, "z_s")
+        dst, src = interleave_views(z_bf[:], z_planes[:])
+        nc.vector.tensor_copy(out=dst, in_=src)
+        nc.vector.quantize_mx(out=z_w[:].bitcast(FP8X4), scales=z_s[:], in_=z_bf[:].rearrange("p c t -> p (c t)"))
+
+        gt_b = g_cols[:, 4:8].unsqueeze(1).to_broadcast([P, CHUNK, PACK])
+        out_rows = out_0.rearrange("(p u) j -> p u j", u=PACK)
+        y_w = tile([P, S], U32, "y_w")
+        y_s = tile([P, S], U8, "y_s")
+        th = [tile([P, CHUNK, PACK], F32, "th%d" % c) for c in range(CHUNKS)]
+        z2_bf = [tile([P, CHUNK, PACK], BF16, "z2_bf%d" % c) for c in range(CHUNKS)]
+        z2_w = [tile([P, CHUNK], U32, "z2_w%d" % c) for c in range(CHUNKS)]
+        z2_s = [tile([P, CHUNK], U8, "z2_s%d" % c) for c in range(CHUNKS)]
+        y = [tile([P, PACK, CHUNK], F32, "y%d" % c) for c in range(CHUNKS)]
+        y_bf = [tile([P, CHUNK, PACK], BF16, "y_bf%d" % c) for c in range(CHUNKS)]
+
+        def scores(c):
+            cols = slice(c * CHUNK, (c + 1) * CHUNK)
+            s_ps = ps.tile([P, PACK, CHUNK], F32, name="s_ps%d" % c, tag="s%d" % c)
+            for t in range(PACK):
+                keys = slice(t * P, (t + 1) * P)
+                mx(s_ps[:, t, :], dk_w[:, keys], dk_plane[:, keys], xq_w[:, cols], xq_s[:, cols])
+            nc.scalar.activation(out=th[c][:], in_=s_ps[:].rearrange("p t n -> p n t"), func=ACT.Tanh, scale=0.0625)
+
+        def weigh(c):
+            nc.vector.tensor_tensor(out=z2_bf[c][:], in0=th[c][:], in1=gt_b, op=MULT)
+
+        def product(c):
+            cols = slice(c * CHUNK, (c + 1) * CHUNK)
+            nc.vector.quantize_mx(
+                out=z2_w[c][:].bitcast(FP8X4), scales=z2_s[c][:], in_=z2_bf[c][:].rearrange("p n t -> p (n t)")
+            )
+            o_ps = ps.tile([P, PACK, CHUNK], F32, name="o_ps%d" % c, tag="v%d" % c)
+            for u in range(PACK):
+                feats = slice(u * P, (u + 1) * P)
+                mx(o_ps[:, u, :], z_w[:, feats], z_s[:, feats], z2_w[c][:], z2_s[c][:])
+            nc.scalar.activation(out=y[c][:], in_=o_ps[:], func=ACT.Copy, scale=0.0625)
+            nc.sync.dma_start(out=out_rows[:, :, cols], in_=y[c][:])
+
+        def round_out(c):
+            dst, src = interleave_views(y_bf[c][:], y[c][:])
+            nc.vector.tensor_copy(out=dst, in_=src)
+
+        def planes(c):
+            cols = slice(c * CHUNK, (c + 1) * CHUNK)
+            nc.vector.quantize_mx(
+                out=y_w[:, cols].bitcast(FP8X4), scales=y_s[:, cols], in_=y_bf[c][:].rearrange("p n t -> p (n t)")
+            )
+
+        for c in range(CHUNKS):
+            scores(c)
+        for step in range(CHUNKS + 3):
+            if step < CHUNKS:
+                weigh(step)
+            if 2 <= step < CHUNKS + 2:
+                round_out(step - 2)
+            if 1 <= step < CHUNKS + 1:
+                product(step - 1)
+            if 3 <= step:
+                planes(step - 3)
+
+        words_out = out_1[0].rearrange("p n t -> p (n t)").bitcast(I32)
+        last = S - CHUNK
+        nc.sync.dma_start(out=words_out[:, 0:last], in_=y_w[:, 0:last].bitcast(I32))
+        nc.sync.dma_start(out=words_out[:, last:S], in_=y_w[:, last:S].bitcast(I32))
+        for q in range(4):
+            eng = nc.scalar if q % 2 else nc.sync
+            eng.dma_start(
+                out=out_2[0, 4 * q : 4 * q + 4, :].bitcast(I32), in_=y_s[32 * q : 32 * q + 4, :].bitcast(I32)
+            )

@@ -52,35 +52,47 @@ def tile_picked_listpq_tanh_po_kernel(
         vidx_t = sb.tile([P, H // 16], U16, name="vidx_t")
         offs_t = sb.tile([P, S // 16], U16, name="offs_t")
         kidx_t = sb.tile([P, H // 16], U16, name="kidx_t")
+        xs_win = tile([P, T], U8, "xs_win")
         ds_win = tile([P, G], U8, "ds_win")
+        xw_win = tile([P, T], U32, "xw_win")
+        dw_win = tile([P, G], U32, "dw_win")
+        wv_raw = [tile([P, PACK, HALF], F32, "wv_raw%d" % h) for h in range(2)]
+        g_rows = tile([P, P], F32, "g_rows")
+        ident = tile([P, P], F32, "ident")
+        dk_plane = tile([P, H], U8, "dk_plane")
+        nc.vector.memset(ds_win[:].bitcast(I32), 0)
+        nc.vector.memset(dk_plane[:].bitcast(I32), 0)
+        nc.gpsimd.memset(g_rows[:], 0.0)
+        make_identity(nc, ident[:])
+
+        wv_rows = wv.rearrange("(p j) c -> p j c", j=PACK)
         nc.sync.dma_start(vidx_t[:], vidx)
         nc.sync.dma_start(offs_t[:], offs)
-        xs_win = tile([P, T], U8, "xs_win")
         for q in range(4):
             rows = x_scales[0, 4 * q : 4 * q + 4, :].bitcast(I32)
             nc.sync.dma_start(
                 out=xs_win[32 * q : 32 * q + 32, :].bitcast(I32),
                 in_=rows.unsqueeze(0).to_broadcast([8, 4, T // 4]),
             )
-        ident = tile([P, P], F32, "ident")
-        wv_raw = tile([P, PACK, N], F32, "wv_raw")
-        xw_win = tile([P, T], U32, "xw_win")
-        dw_win = tile([P, G], U32, "dw_win")
-        nc.sync.dma_start(out=wv_raw[:], in_=wv.rearrange("(p j) c -> p j c", j=PACK))
         nc.sync.dma_start(out=xw_win[:].bitcast(I32), in_=x_words[0].rearrange("p n t -> p (n t)").bitcast(I32))
+        nc.sync.dma_start(out=wv_raw[0][:], in_=wv_rows[:, :, 0:HALF])
         nc.sync.dma_start(kidx_t[:], kidx)
-        nc.sync.dma_start(out=dw_win[:].bitcast(I32), in_=d_words[0].rearrange("p n t -> p (n t)").bitcast(I32))
-        nc.vector.memset(ds_win[:].bitcast(I32), 0)
-        nc.gpsimd.dma_start(out=ds_win[0:P:8, :].bitcast(I32), in_=d_scales[0].bitcast(I32))
-
-        g_rows = tile([P, P], F32, "g_rows")
-        nc.gpsimd.memset(g_rows[:], 0.0)
+        nc.sync.dma_start(out=ds_win[0:P:8, :].bitcast(I32), in_=d_scales[0].bitcast(I32))
         for r, vec in enumerate((gi, gt)):
-            nc.gpsimd.dma_start(
+            nc.sync.dma_start(
                 out=g_rows[4 * r : 4 * r + 4, :].rearrange("t (q r) -> t q r", r=8),
                 in_=vec.rearrange("(q t r) o -> t q (r o)", t=4, r=8),
             )
-        make_identity(nc, ident[:])
+        nc.sync.dma_start(out=wv_raw[1][:], in_=wv_rows[:, :, HALF:N])
+        nc.sync.dma_start(out=dw_win[:].bitcast(I32), in_=d_words[0].rearrange("p n t -> p (n t)").bitcast(I32))
+
+        wv_bf = [sb.tile([P, HALF, PACK], BF16, name="wv_bf%d" % h, tag="reuse%d" % h, align_bytes=64) for h in range(2)]
+        wv_w = tile([P, N], U32, "wv_w")
+        wv_s = tile([P, N], U8, "wv_s")
+        for h in range(2):
+            dst, src = interleave_views(wv_bf[h][:], wv_raw[h][:])
+            nc.scalar.copy(out=dst, in_=src)
+
         g_ps = ps.tile([P, P], F32, name="g_ps", tag="s3")
         nc.tensor.transpose(g_ps[:], g_rows[:], ident[:])
         g_cols = tile([P, 8], F32, "g_cols")
@@ -91,28 +103,23 @@ def tile_picked_listpq_tanh_po_kernel(
         xq_s = tile([P, S], U8, "xq_s")
         dk_s_raw = tile([P, H], U8, "dk_s_raw")
         dk_s = tile([P, H], U8, "dk_s")
-        dk_plane = tile([P, H], U8, "dk_plane")
-        nc.vector.memset(dk_plane[:].bitcast(I32), 0)
+        xv_w = tile([P, H], U32, "xv_w")
+        dk_w = tile([P, H], U32, "dk_w")
         nc.vector.tensor_copy(xv_s_raw[:], xs_win[:].indirect(vidx_t[:]))
         nc.vector.tensor_copy(xq_s[:], xs_win[:].indirect(offs_t[:]))
         deal_scales(xv_s, xv_s_raw)
-
-        wv_bf = tile([P, N, PACK], BF16, "wv_bf")
-        wv_w = tile([P, N], U32, "wv_w")
-        wv_s = tile([P, N], U8, "wv_s")
-        dst, src = interleave_views(wv_bf[:], wv_raw[:])
-        nc.scalar.copy(out=dst, in_=src)
-
-        xv_w = tile([P, H], U32, "xv_w")
-        xq_w = tile([P, S], U32, "xq_w")
-        dk_w_raw = tile([P, H], U32, "dk_w_raw")
-        dk_w = tile([P, H], U32, "dk_w")
         nc.vector.tensor_copy(xv_w[:].rearrange("p (t q r) -> p q t r", t=4, r=8), xw_win[:].indirect(vidx_t[:]))
-        nc.vector.quantize_mx(out=wv_w[:].bitcast(FP8X4), scales=wv_s[:], in_=wv_bf[:].rearrange("p c t -> p (c t)"))
         nc.vector.tensor_copy(dk_s_raw[:], ds_win[:].indirect(kidx_t[:]))
         deal_scales(dk_s, dk_s_raw)
         for j in range(4):
             nc.sync.dma_start(out=dk_plane[j:P:32, :].bitcast(I32), in_=dk_s[8 * j : P : 32, :].bitcast(I32))
+        for h in range(2):
+            cols = slice(h * HALF, (h + 1) * HALF)
+            nc.vector.quantize_mx(
+                out=wv_w[:, cols].bitcast(FP8X4), scales=wv_s[:, cols], in_=wv_bf[h][:].rearrange("p c t -> p (c t)")
+            )
+        xq_w = sb.tile([P, S], U32, name="xq_w", tag="reuse0", align_bytes=64)
+        dk_w_raw = sb.tile([P, H], U32, name="dk_w_raw", tag="reuse1", align_bytes=64)
         nc.vector.tensor_copy(xq_w[:], xw_win[:].indirect(offs_t[:]))
         nc.vector.tensor_copy(dk_w_raw[:], dw_win[:].indirect(kidx_t[:]))
         nc.vector.tensor_copy(
@@ -121,21 +128,27 @@ def tile_picked_listpq_tanh_po_kernel(
         )
 
         z_planes = tile([P, PACK, N], BF16, "z_planes")
-        for t in range(PACK):
-            keys = slice(t * P, (t + 1) * P)
-            val = ps.tile([P, N], F32, name="val%d" % t, tag="v%d" % t)
-            mx(val[:], xv_w[:, keys], xv_s[:, keys], wv_w[:], wv_s[:])
-            nc.scalar.activation(
-                out=z_planes[:, t, :].rearrange("p (u m) -> p u m", u=PACK),
-                in_=val[:].rearrange("p (m u) -> p u m", u=PACK),
-                func=ACT.Copy, scale=g_cols[:, t : t + 1],
-            )
+        z_dealt = z_planes[:].rearrange("p t (u h m) -> p t h u m", u=PACK, h=2)
+        for h in range(2):
+            cols = slice(h * HALF, (h + 1) * HALF)
+            for pair in range(2):
+                val = ps.tile([P, 2, HALF], F32, name="val%d%d" % (h, pair), tag="v%d" % (2 * h + pair))
+                for e in range(2):
+                    keys = slice((2 * pair + e) * P, (2 * pair + e + 1) * P)
+                    mx(val[:, e, :], xv_w[:, keys], xv_s[:, keys], wv_w[:, cols], wv_s[:, cols])
+                for e in range(2):
+                    t = 2 * pair + e
+                    nc.scalar.activation(
+                        out=z_dealt[:, t, h], in_=val[:, e, :].rearrange("p (m u) -> p u m", u=PACK),
+                        func=ACT.Copy, scale=g_cols[:, t : t + 1],
+                    )
         z_bf = tile([P, N, PACK], BF16, "z_bf")
         z_w = tile([P, N], U32, "z_w")
         z_s = tile([P, N], U8, "z_s")
-        dst, src = interleave_views(z_bf[:], z_planes[:])
+        dst, src = interleave_views(z_bf[:, 0:P, :], z_planes[:, :, 0:P])
+        nc.scalar.copy(out=dst, in_=src)
+        dst, src = interleave_views(z_bf[:, P:N, :], z_planes[:, :, P:N])
         nc.vector.tensor_copy(out=dst, in_=src)
-        nc.vector.quantize_mx(out=z_w[:].bitcast(FP8X4), scales=z_s[:], in_=z_bf[:].rearrange("p c t -> p (c t)"))
 
         gt_b = g_cols[:, 4:8].unsqueeze(1).to_broadcast([P, CHUNK, PACK])
         out_rows = out_0.rearrange("(p u) j -> p u j", u=PACK)
@@ -183,20 +196,22 @@ def tile_picked_listpq_tanh_po_kernel(
 
         for c in range(CHUNKS):
             scores(c)
-        for step in range(CHUNKS + 3):
-            if step < CHUNKS:
-                weigh(step)
-            if 2 <= step < CHUNKS + 2:
-                round_out(step - 2)
-            if 1 <= step < CHUNKS + 1:
-                product(step - 1)
-            if 3 <= step:
-                planes(step - 3)
+        weigh(0)
+        nc.vector.quantize_mx(out=z_w[:].bitcast(FP8X4), scales=z_s[:], in_=z_bf[:].rearrange("p c t -> p (c t)"))
+        for c in range(CHUNKS):
+            if c + 1 < CHUNKS:
+                weigh(c + 1)
+            product(c)
+        round_out(0)
+        for c in range(CHUNKS):
+            if c + 1 < CHUNKS:
+                round_out(c + 1)
+            planes(c)
 
         words_out = out_1[0].rearrange("p n t -> p (n t)").bitcast(I32)
         last = S - CHUNK
         nc.sync.dma_start(out=words_out[:, 0:last], in_=y_w[:, 0:last].bitcast(I32))
-        nc.sync.dma_start(out=words_out[:, last:S], in_=y_w[:, last:S].bitcast(I32))
+        nc.scalar.dma_start(out=words_out[:, last:S], in_=y_w[:, last:S].bitcast(I32))
         for q in range(4):
             eng = nc.scalar if q % 2 else nc.sync
             eng.dma_start(

@@ -4,7 +4,7 @@ import concourse.mybir as mybir
 from concourse.masks import make_identity
 
 K, T, S, N, G, H = 512, 2048, 512, 512, 2048, 512
-FLOPS = 3 * 2 * 512 * 512 * 512
+FLOPS = 2 * K * H * N + 2 * K * H * S + 2 * H * N * S
 
 F32 = mybir.dt.float32
 BF16 = mybir.dt.bfloat16
@@ -18,9 +18,15 @@ MULT = mybir.AluOpType.mult
 
 P = 128
 PACK = 4
+BLOCK_PARTS = 8
+QUADRANT = 32
+LIST_PARTS = 16
+SIXTEENTH = 0.0625
+HALF = N // 2
 CHUNK = 128
 CHUNKS = S // CHUNK
-HALF = N // 2
+SPANS = ((0, 2), (2, 3), (3, 4))
+Z_ON_SCALAR = P
 
 
 def tile_picked_listpq_tanh_po_kernel(
@@ -31,27 +37,36 @@ def tile_picked_listpq_tanh_po_kernel(
         sb = ctx.enter_context(tc.tile_pool(name="sb", bufs=1))
         ps = ctx.enter_context(tc.psum_pool(name="ps", bufs=1))
 
-        def tile(shape, dtype, name):
-            return sb.tile(shape, dtype, name=name, align_bytes=64)
+        def tile(shape, dtype, name, tag=""):
+            return sb.tile(shape, dtype, name=name, tag=tag, align_bytes=64)
 
-        def mx(out, lhs_words, lhs_scales, rhs_words, rhs_scales):
+        def matmul(out, lhs_words, lhs_scales, rhs_words, rhs_scales):
             nc.tensor.matmul_mx(
                 out=out, lhsT=lhs_words.bitcast(FP8X4), lhsT_scale=lhs_scales,
                 rhs=rhs_words.bitcast(FP8X4), rhs_scale=rhs_scales, start=True, stop=True,
             )
 
+        def quantise(words, scales, values):
+            nc.vector.quantize_mx(out=words.bitcast(FP8X4), scales=scales, in_=values.rearrange("p c b -> p (c b)"))
+
         def interleave_views(dst, src):
-            return (dst.rearrange("p (c i) t -> p c t i", i=4), src.rearrange("p t (c i) -> p c t i", i=4))
+            return (dst.rearrange("p (c i) b -> p c b i", i=4), src.rearrange("p b (c i) -> p c b i", i=4))
 
         def deal_scales(dst, src):
             nc.vector.tensor_copy(
-                out=dst[:].bitcast(I32).rearrange("p (t q w) -> p q t w", t=4, w=2),
-                in_=src[:].bitcast(I32).rearrange("p (q t w) -> p q t w", t=4, w=2),
+                out=dst[:].bitcast(I32).rearrange("p (t a w) -> p a t w", t=PACK, w=2),
+                in_=src[:].bitcast(I32).rearrange("p (a t w) -> p a t w", t=PACK, w=2),
             )
 
-        vidx_t = sb.tile([P, H // 16], U16, name="vidx_t")
-        offs_t = sb.tile([P, S // 16], U16, name="offs_t")
-        kidx_t = sb.tile([P, H // 16], U16, name="kidx_t")
+        def dealt(words):
+            return words.rearrange("p (t a r) -> p a t r", t=PACK, r=BLOCK_PARTS)
+
+        def word_rows(dram_words):
+            return dram_words[0].rearrange("p n b -> p (n b)").bitcast(I32)
+
+        vidx_t = sb.tile([P, H // LIST_PARTS], U16, name="vidx_t")
+        offs_t = sb.tile([P, S // LIST_PARTS], U16, name="offs_t")
+        kidx_t = sb.tile([P, H // LIST_PARTS], U16, name="kidx_t")
         xs_win = tile([P, T], U8, "xs_win")
         ds_win = tile([P, G], U8, "ds_win")
         xw_win = tile([P, T], U32, "xw_win")
@@ -65,38 +80,38 @@ def tile_picked_listpq_tanh_po_kernel(
         nc.gpsimd.memset(g_rows[:], 0.0)
         make_identity(nc, ident[:])
 
-        wv_rows = wv.rearrange("(p j) c -> p j c", j=PACK)
+        wv_rows = wv.rearrange("(p b) c -> p b c", b=PACK)
         nc.sync.dma_start(vidx_t[:], vidx)
         nc.sync.dma_start(offs_t[:], offs)
-        for q in range(4):
+        for q in range(P // QUADRANT):
             rows = x_scales[0, 4 * q : 4 * q + 4, :].bitcast(I32)
             nc.sync.dma_start(
-                out=xs_win[32 * q : 32 * q + 32, :].bitcast(I32),
-                in_=rows.unsqueeze(0).to_broadcast([8, 4, T // 4]),
+                out=xs_win[QUADRANT * q : QUADRANT * (q + 1), :].bitcast(I32),
+                in_=rows.unsqueeze(0).to_broadcast([QUADRANT // 4, 4, T // 4]),
             )
-        nc.sync.dma_start(out=xw_win[:].bitcast(I32), in_=x_words[0].rearrange("p n t -> p (n t)").bitcast(I32))
+        nc.sync.dma_start(out=xw_win[:].bitcast(I32), in_=word_rows(x_words))
         nc.sync.dma_start(out=wv_raw[0][:], in_=wv_rows[:, :, 0:HALF])
         nc.sync.dma_start(kidx_t[:], kidx)
-        nc.sync.dma_start(out=ds_win[0:P:8, :].bitcast(I32), in_=d_scales[0].bitcast(I32))
-        for r, vec in enumerate((gi, gt)):
+        nc.sync.dma_start(out=ds_win[0:P:BLOCK_PARTS, :].bitcast(I32), in_=d_scales[0].bitcast(I32))
+        for v, vec in enumerate((gi, gt)):
             nc.sync.dma_start(
-                out=g_rows[4 * r : 4 * r + 4, :].rearrange("t (q r) -> t q r", r=8),
-                in_=vec.rearrange("(q t r) o -> t q (r o)", t=4, r=8),
+                out=g_rows[PACK * v : PACK * (v + 1), :].rearrange("t (a r) -> t a r", r=BLOCK_PARTS),
+                in_=vec.rearrange("(a t r) o -> t a (r o)", t=PACK, r=BLOCK_PARTS),
             )
         nc.sync.dma_start(out=wv_raw[1][:], in_=wv_rows[:, :, HALF:N])
-        nc.sync.dma_start(out=dw_win[:].bitcast(I32), in_=d_words[0].rearrange("p n t -> p (n t)").bitcast(I32))
+        nc.sync.dma_start(out=dw_win[:].bitcast(I32), in_=word_rows(d_words))
 
-        wv_bf = [sb.tile([P, HALF, PACK], BF16, name="wv_bf%d" % h, tag="reuse%d" % h, align_bytes=64) for h in range(2)]
+        wv_bf = [tile([P, HALF, PACK], BF16, "wv_bf%d" % h, tag="reuse%d" % h) for h in range(2)]
         wv_w = tile([P, N], U32, "wv_w")
         wv_s = tile([P, N], U8, "wv_s")
         for h in range(2):
             dst, src = interleave_views(wv_bf[h][:], wv_raw[h][:])
             nc.scalar.copy(out=dst, in_=src)
 
-        g_ps = ps.tile([P, P], F32, name="g_ps", tag="s3")
+        g_ps = ps.tile([P, P], F32, name="g_ps", tag="score%d" % (CHUNKS - 1))
         nc.tensor.transpose(g_ps[:], g_rows[:], ident[:])
-        g_cols = tile([P, 8], F32, "g_cols")
-        nc.scalar.copy(out=g_cols[:], in_=g_ps[:, 0:8])
+        g_cols = tile([P, 2 * PACK], F32, "g_cols")
+        nc.scalar.copy(out=g_cols[:], in_=g_ps[:, 0 : 2 * PACK])
 
         xv_s_raw = tile([P, H], U8, "xv_s_raw")
         xv_s = tile([P, H], U8, "xv_s")
@@ -108,49 +123,48 @@ def tile_picked_listpq_tanh_po_kernel(
         nc.vector.tensor_copy(xv_s_raw[:], xs_win[:].indirect(vidx_t[:]))
         nc.vector.tensor_copy(xq_s[:], xs_win[:].indirect(offs_t[:]))
         deal_scales(xv_s, xv_s_raw)
-        nc.vector.tensor_copy(xv_w[:].rearrange("p (t q r) -> p q t r", t=4, r=8), xw_win[:].indirect(vidx_t[:]))
+        nc.vector.tensor_copy(dealt(xv_w[:]), xw_win[:].indirect(vidx_t[:]))
         nc.vector.tensor_copy(dk_s_raw[:], ds_win[:].indirect(kidx_t[:]))
         deal_scales(dk_s, dk_s_raw)
         for j in range(4):
-            nc.sync.dma_start(out=dk_plane[j:P:32, :].bitcast(I32), in_=dk_s[8 * j : P : 32, :].bitcast(I32))
+            nc.sync.dma_start(
+                out=dk_plane[j:P:QUADRANT, :].bitcast(I32), in_=dk_s[BLOCK_PARTS * j : P : QUADRANT, :].bitcast(I32)
+            )
         for h in range(2):
             cols = slice(h * HALF, (h + 1) * HALF)
-            nc.vector.quantize_mx(
-                out=wv_w[:, cols].bitcast(FP8X4), scales=wv_s[:, cols], in_=wv_bf[h][:].rearrange("p c t -> p (c t)")
-            )
-        xq_w = sb.tile([P, S], U32, name="xq_w", tag="reuse0", align_bytes=64)
-        dk_w_raw = sb.tile([P, H], U32, name="dk_w_raw", tag="reuse1", align_bytes=64)
+            quantise(wv_w[:, cols], wv_s[:, cols], wv_bf[h][:])
+        xq_w = tile([P, S], U32, "xq_w", tag="reuse0")
+        dk_w_raw = tile([P, H], U32, "dk_w_raw", tag="reuse1")
         nc.vector.tensor_copy(xq_w[:], xw_win[:].indirect(offs_t[:]))
         nc.vector.tensor_copy(dk_w_raw[:], dw_win[:].indirect(kidx_t[:]))
         nc.vector.tensor_copy(
-            out=dk_w[:].rearrange("p (t q r) -> p q t r", t=4, r=8),
-            in_=dk_w_raw[:].rearrange("p (q t r) -> p q t r", t=4, r=8),
+            out=dealt(dk_w[:]), in_=dk_w_raw[:].rearrange("p (a t r) -> p a t r", t=PACK, r=BLOCK_PARTS)
         )
 
-        z_planes = tile([P, PACK, N], BF16, "z_planes")
-        z_dealt = z_planes[:].rearrange("p t (u h m) -> p t h u m", u=PACK, h=2)
+        z_tiles = tile([P, PACK, N], BF16, "z_tiles")
+        z_by_half = z_tiles[:].rearrange("p t (u h f) -> p t h u f", u=PACK, h=2)
         for h in range(2):
             cols = slice(h * HALF, (h + 1) * HALF)
             for pair in range(2):
-                val = ps.tile([P, 2, HALF], F32, name="val%d%d" % (h, pair), tag="v%d" % (2 * h + pair))
+                val = ps.tile([P, 2, HALF], F32, name="val%d%d" % (h, pair), tag="value%d" % (2 * h + pair))
                 for e in range(2):
                     keys = slice((2 * pair + e) * P, (2 * pair + e + 1) * P)
-                    mx(val[:, e, :], xv_w[:, keys], xv_s[:, keys], wv_w[:, cols], wv_s[:, cols])
+                    matmul(val[:, e, :], xv_w[:, keys], xv_s[:, keys], wv_w[:, cols], wv_s[:, cols])
                 for e in range(2):
                     t = 2 * pair + e
                     nc.scalar.activation(
-                        out=z_dealt[:, t, h], in_=val[:, e, :].rearrange("p (m u) -> p u m", u=PACK),
+                        out=z_by_half[:, t, h], in_=val[:, e, :].rearrange("p (f u) -> p u f", u=PACK),
                         func=ACT.Copy, scale=g_cols[:, t : t + 1],
                     )
         z_bf = tile([P, N, PACK], BF16, "z_bf")
         z_w = tile([P, N], U32, "z_w")
         z_s = tile([P, N], U8, "z_s")
-        dst, src = interleave_views(z_bf[:, 0:P, :], z_planes[:, :, 0:P])
+        dst, src = interleave_views(z_bf[:, 0:Z_ON_SCALAR, :], z_tiles[:, :, 0:Z_ON_SCALAR])
         nc.scalar.copy(out=dst, in_=src)
-        dst, src = interleave_views(z_bf[:, P:N, :], z_planes[:, :, P:N])
+        dst, src = interleave_views(z_bf[:, Z_ON_SCALAR:N, :], z_tiles[:, :, Z_ON_SCALAR:N])
         nc.vector.tensor_copy(out=dst, in_=src)
 
-        gt_b = g_cols[:, 4:8].unsqueeze(1).to_broadcast([P, CHUNK, PACK])
+        gt_b = g_cols[:, PACK : 2 * PACK].unsqueeze(1).to_broadcast([P, CHUNK, PACK])
         out_rows = out_0.rearrange("(p u) j -> p u j", u=PACK)
         y_w = tile([P, S], U32, "y_w")
         y_s = tile([P, S], U8, "y_s")
@@ -158,62 +172,60 @@ def tile_picked_listpq_tanh_po_kernel(
         z2_bf = [tile([P, CHUNK, PACK], BF16, "z2_bf%d" % c) for c in range(CHUNKS)]
         z2_w = [tile([P, CHUNK], U32, "z2_w%d" % c) for c in range(CHUNKS)]
         z2_s = [tile([P, CHUNK], U8, "z2_s%d" % c) for c in range(CHUNKS)]
-        y = [tile([P, PACK, CHUNK], F32, "y%d" % c) for c in range(CHUNKS)]
-        y_bf = [tile([P, CHUNK, PACK], BF16, "y_bf%d" % c) for c in range(CHUNKS)]
+        y = [tile([P, PACK, (hi - lo) * CHUNK], F32, "y%d" % lo) for lo, hi in SPANS]
+        y_bf = [tile([P, (hi - lo) * CHUNK, PACK], BF16, "y_bf%d" % lo) for lo, hi in SPANS]
+        span_of = [n for n, (lo, hi) in enumerate(SPANS) for c in range(lo, hi)]
 
         def scores(c):
             cols = slice(c * CHUNK, (c + 1) * CHUNK)
-            s_ps = ps.tile([P, PACK, CHUNK], F32, name="s_ps%d" % c, tag="s%d" % c)
+            s_ps = ps.tile([P, PACK, CHUNK], F32, name="s_ps%d" % c, tag="score%d" % c)
             for t in range(PACK):
                 keys = slice(t * P, (t + 1) * P)
-                mx(s_ps[:, t, :], dk_w[:, keys], dk_plane[:, keys], xq_w[:, cols], xq_s[:, cols])
-            nc.scalar.activation(out=th[c][:], in_=s_ps[:].rearrange("p t n -> p n t"), func=ACT.Tanh, scale=0.0625)
+                matmul(s_ps[:, t, :], dk_w[:, keys], dk_plane[:, keys], xq_w[:, cols], xq_s[:, cols])
+            nc.scalar.activation(out=th[c][:], in_=s_ps[:].rearrange("p t j -> p j t"), func=ACT.Tanh, scale=SIXTEENTH)
 
         def weigh(c):
             nc.vector.tensor_tensor(out=z2_bf[c][:], in0=th[c][:], in1=gt_b, op=MULT)
 
         def product(c):
-            cols = slice(c * CHUNK, (c + 1) * CHUNK)
-            nc.vector.quantize_mx(
-                out=z2_w[c][:].bitcast(FP8X4), scales=z2_s[c][:], in_=z2_bf[c][:].rearrange("p n t -> p (n t)")
-            )
-            o_ps = ps.tile([P, PACK, CHUNK], F32, name="o_ps%d" % c, tag="v%d" % c)
+            quantise(z2_w[c][:], z2_s[c][:], z2_bf[c][:])
+            o_ps = ps.tile([P, PACK, CHUNK], F32, name="o_ps%d" % c, tag="value%d" % c)
             for u in range(PACK):
                 feats = slice(u * P, (u + 1) * P)
-                mx(o_ps[:, u, :], z_w[:, feats], z_s[:, feats], z2_w[c][:], z2_s[c][:])
-            nc.scalar.activation(out=y[c][:], in_=o_ps[:], func=ACT.Copy, scale=0.0625)
-            nc.sync.dma_start(out=out_rows[:, :, cols], in_=y[c][:])
-
-        def round_out(c):
-            dst, src = interleave_views(y_bf[c][:], y[c][:])
-            nc.vector.tensor_copy(out=dst, in_=src)
-
-        def planes(c):
-            cols = slice(c * CHUNK, (c + 1) * CHUNK)
-            nc.vector.quantize_mx(
-                out=y_w[:, cols].bitcast(FP8X4), scales=y_s[:, cols], in_=y_bf[c][:].rearrange("p n t -> p (n t)")
-            )
+                matmul(o_ps[:, u, :], z_w[:, feats], z_s[:, feats], z2_w[c][:], z2_s[c][:])
+            span = span_of[c]
+            first = (c - SPANS[span][0]) * CHUNK
+            y_part = y[span][:, :, first : first + CHUNK]
+            nc.scalar.activation(out=y_part, in_=o_ps[:], func=ACT.Copy, scale=SIXTEENTH)
+            nc.sync.dma_start(out=out_rows[:, :, c * CHUNK : (c + 1) * CHUNK], in_=y_part)
+            if c == CHUNKS - 1:
+                nc.scalar.activation(
+                    out=y_bf[span][:], in_=o_ps[:].rearrange("p u j -> p j u"), func=ACT.Copy, scale=SIXTEENTH
+                )
 
         for c in range(CHUNKS):
             scores(c)
         weigh(0)
-        nc.vector.quantize_mx(out=z_w[:].bitcast(FP8X4), scales=z_s[:], in_=z_bf[:].rearrange("p c t -> p (c t)"))
+        quantise(z_w[:], z_s[:], z_bf[:])
         for c in range(CHUNKS):
             if c + 1 < CHUNKS:
                 weigh(c + 1)
             product(c)
-        round_out(0)
-        for c in range(CHUNKS):
-            if c + 1 < CHUNKS:
-                round_out(c + 1)
-            planes(c)
 
-        words_out = out_1[0].rearrange("p n t -> p (n t)").bitcast(I32)
+        for span in range(len(SPANS) - 1):
+            dst, src = interleave_views(y_bf[span][:], y[span][:])
+            nc.vector.tensor_copy(out=dst, in_=src)
+        for span, (lo, hi) in enumerate(SPANS):
+            cols = slice(lo * CHUNK, hi * CHUNK)
+            quantise(y_w[:, cols], y_s[:, cols], y_bf[span][:])
+
+        words_out = word_rows(out_1)
         last = S - CHUNK
         nc.sync.dma_start(out=words_out[:, 0:last], in_=y_w[:, 0:last].bitcast(I32))
-        nc.scalar.dma_start(out=words_out[:, last:S], in_=y_w[:, last:S].bitcast(I32))
-        for q in range(4):
-            eng = nc.scalar if q % 2 else nc.sync
-            eng.dma_start(
-                out=out_2[0, 4 * q : 4 * q + 4, :].bitcast(I32), in_=y_s[32 * q : 32 * q + 4, :].bitcast(I32)
+        nc.sync.dma_start(out=words_out[:, last:S], in_=y_w[:, last:S].bitcast(I32))
+        for q in range(P // QUADRANT):
+            queue = nc.scalar if q % 2 else nc.sync
+            queue.dma_start(
+                out=out_2[0, 4 * q : 4 * q + 4, :].bitcast(I32),
+                in_=y_s[QUADRANT * q : QUADRANT * q + 4, :].bitcast(I32),
             )

@@ -35,6 +35,7 @@ def tile_picked_listpq_tanh_po_kernel(
     nc = tc.nc
     with ExitStack() as ctx:
         sb = ctx.enter_context(tc.tile_pool(name="sb", bufs=1))
+        shared = ctx.enter_context(tc.tile_pool(name="shared", bufs=1))
         ps = ctx.enter_context(tc.psum_pool(name="ps", bufs=1))
 
         def tile(shape, dtype, name, tag=""):
@@ -101,7 +102,10 @@ def tile_picked_listpq_tanh_po_kernel(
         nc.sync.dma_start(out=wv_raw[1][:], in_=wv_rows[:, :, HALF:N])
         nc.sync.dma_start(out=dw_win[:].bitcast(I32), in_=word_rows(d_words))
 
-        wv_bf = [tile([P, HALF, PACK], BF16, "wv_bf%d" % h, tag="reuse%d" % h) for h in range(2)]
+        wv_bf = [
+            shared.tile([P, HALF, PACK], BF16, name="wv_bf0", offset=0, align_bytes=64),
+            tile([P, HALF, PACK], BF16, "wv_bf1", tag="wv_bf1_bytes"),
+        ]
         wv_w = tile([P, N], U32, "wv_w")
         wv_s = tile([P, N], U8, "wv_s")
         for h in range(2):
@@ -117,7 +121,6 @@ def tile_picked_listpq_tanh_po_kernel(
         xv_s = tile([P, H], U8, "xv_s")
         xq_s = tile([P, S], U8, "xq_s")
         dk_s_raw = tile([P, H], U8, "dk_s_raw")
-        dk_s = tile([P, H], U8, "dk_s")
         xv_w = tile([P, H], U32, "xv_w")
         dk_w = tile([P, H], U32, "dk_w")
         nc.vector.tensor_copy(xv_s_raw[:], xs_win[:].indirect(vidx_t[:]))
@@ -125,16 +128,16 @@ def tile_picked_listpq_tanh_po_kernel(
         deal_scales(xv_s, xv_s_raw)
         nc.vector.tensor_copy(dealt(xv_w[:]), xw_win[:].indirect(vidx_t[:]))
         nc.vector.tensor_copy(dk_s_raw[:], ds_win[:].indirect(kidx_t[:]))
+        quantise(wv_w[:, 0:HALF], wv_s[:, 0:HALF], wv_bf[0][:])
+        dk_s = shared.tile([P, H], U8, name="dk_s", offset=0, align_bytes=64)
         deal_scales(dk_s, dk_s_raw)
         for j in range(4):
             nc.sync.dma_start(
                 out=dk_plane[j:P:QUADRANT, :].bitcast(I32), in_=dk_s[BLOCK_PARTS * j : P : QUADRANT, :].bitcast(I32)
             )
-        for h in range(2):
-            cols = slice(h * HALF, (h + 1) * HALF)
-            quantise(wv_w[:, cols], wv_s[:, cols], wv_bf[h][:])
-        xq_w = tile([P, S], U32, "xq_w", tag="reuse0")
-        dk_w_raw = tile([P, H], U32, "dk_w_raw", tag="reuse1")
+        quantise(wv_w[:, HALF:N], wv_s[:, HALF:N], wv_bf[1][:])
+        xq_w = shared.tile([P, S], U32, name="xq_w", offset=H, align_bytes=64)
+        dk_w_raw = tile([P, H], U32, "dk_w_raw", tag="wv_bf1_bytes")
         nc.vector.tensor_copy(xq_w[:], xw_win[:].indirect(offs_t[:]))
         nc.vector.tensor_copy(dk_w_raw[:], dw_win[:].indirect(kidx_t[:]))
         nc.vector.tensor_copy(

from contextlib import ExitStack

import concourse.mybir as mybir
from concourse.masks import make_identity

K, T, S, N, G, H = 512, 2048, 512, 512, 2048, 512
FLOPS = 2 * K * H * N + 2 * K * H * S + 2 * H * N * S

F32 = mybir.dt.float32
BF16 = mybir.dt.bfloat16
U32 = mybir.dt.uint32
I32 = mybir.dt.int32
U16 = mybir.dt.uint16
U8 = mybir.dt.uint8
FP8X4 = mybir.dt.float8_e4m3fn_x4
ACT = mybir.ActivationFunctionType
MULT = mybir.AluOpType.mult

P = 128
PACK = 4
BLOCK_PARTS = 8
QUADRANT = 32
LIST_PARTS = 16
SIXTEENTH = 0.0625
HALF = N // 2
CHUNK = 128
CHUNKS = S // CHUNK
SPANS = ((0, 2), (2, 3), (3, 4))
Z_ON_SCALAR = P


def tile_picked_listpq_tanh_po_kernel(
    tc, x_words, x_scales, d_words, d_scales, wv, gi, gt, offs, kidx, vidx, out_0, out_1, out_2
):
    nc = tc.nc
    with ExitStack() as ctx:
        sb = ctx.enter_context(tc.tile_pool(name="sb", bufs=1))
        shared = ctx.enter_context(tc.tile_pool(name="shared", bufs=1))
        ps = ctx.enter_context(tc.psum_pool(name="ps", bufs=1))

        def tile(shape, dtype, name, tag=""):
            return sb.tile(shape, dtype, name=name, tag=tag, align_bytes=64)

        def matmul(out, lhs_words, lhs_scales, rhs_words, rhs_scales):
            nc.tensor.matmul_mx(
                out=out, lhsT=lhs_words.bitcast(FP8X4), lhsT_scale=lhs_scales,
                rhs=rhs_words.bitcast(FP8X4), rhs_scale=rhs_scales, start=True, stop=True,
            )

        def quantise(words, scales, values):
            nc.vector.quantize_mx(out=words.bitcast(FP8X4), scales=scales, in_=values.rearrange("p c b -> p (c b)"))

        def interleave_views(dst, src):
            return (dst.rearrange("p (c i) b -> p c b i", i=4), src.rearrange("p b (c i) -> p c b i", i=4))

        def deal_scales(dst, src):
            nc.vector.tensor_copy(
                out=dst[:].bitcast(I32).rearrange("p (t a w) -> p a t w", t=PACK, w=2),
                in_=src[:].bitcast(I32).rearrange("p (a t w) -> p a t w", t=PACK, w=2),
            )

        def dealt(words):
            return words.rearrange("p (t a r) -> p a t r", t=PACK, r=BLOCK_PARTS)

        def word_rows(dram_words):
            return dram_words[0].rearrange("p n b -> p (n b)").bitcast(I32)

        vidx_t = sb.tile([P, H // LIST_PARTS], U16, name="vidx_t")
        offs_t = sb.tile([P, S // LIST_PARTS], U16, name="offs_t")
        kidx_t = sb.tile([P, H // LIST_PARTS], U16, name="kidx_t")
        xs_win = tile([P, T], U8, "xs_win")
        ds_win = tile([P, G], U8, "ds_win")
        xw_win = tile([P, T], U32, "xw_win")
        dw_win = tile([P, G], U32, "dw_win")
        wv_raw = [tile([P, PACK, HALF], F32, "wv_raw%d" % h) for h in range(2)]
        g_rows = tile([P, P], F32, "g_rows")
        ident = tile([P, P], F32, "ident")
        dk_plane = tile([P, H], U8, "dk_plane")
        nc.vector.memset(ds_win[:].bitcast(I32), 0)
        nc.vector.memset(dk_plane[:].bitcast(I32), 0)
        nc.gpsimd.memset(g_rows[:], 0.0)
        make_identity(nc, ident[:])

        wv_rows = wv.rearrange("(p b) c -> p b c", b=PACK)
        nc.sync.dma_start(vidx_t[:], vidx)
        nc.sync.dma_start(offs_t[:], offs)
        for q in range(P // QUADRANT):
            rows = x_scales[0, 4 * q : 4 * q + 4, :].bitcast(I32)
            nc.sync.dma_start(
                out=xs_win[QUADRANT * q : QUADRANT * (q + 1), :].bitcast(I32),
                in_=rows.unsqueeze(0).to_broadcast([QUADRANT // 4, 4, T // 4]),
            )
        nc.sync.dma_start(out=xw_win[:].bitcast(I32), in_=word_rows(x_words))
        nc.sync.dma_start(out=wv_raw[0][:], in_=wv_rows[:, :, 0:HALF])
        nc.sync.dma_start(kidx_t[:], kidx)
        nc.sync.dma_start(out=ds_win[0:P:BLOCK_PARTS, :].bitcast(I32), in_=d_scales[0].bitcast(I32))
        for v, vec in enumerate((gi, gt)):
            nc.sync.dma_start(
                out=g_rows[PACK * v : PACK * (v + 1), :].rearrange("t (a r) -> t a r", r=BLOCK_PARTS),
                in_=vec.rearrange("(a t r) o -> t a (r o)", t=PACK, r=BLOCK_PARTS),
            )
        nc.sync.dma_start(out=wv_raw[1][:], in_=wv_rows[:, :, HALF:N])
        nc.sync.dma_start(out=dw_win[:].bitcast(I32), in_=word_rows(d_words))

        wv_bf = [
            shared.tile([P, HALF, PACK], BF16, name="wv_bf0", offset=0, align_bytes=64),
            tile([P, HALF, PACK], BF16, "wv_bf1", tag="wv_bf1_bytes"),
        ]
        wv_w = tile([P, N], U32, "wv_w")
        wv_s = tile([P, N], U8, "wv_s")
        for h in range(2):
            dst, src = interleave_views(wv_bf[h][:], wv_raw[h][:])
            nc.scalar.copy(out=dst, in_=src)

        g_ps = ps.tile([P, P], F32, name="g_ps", tag="score%d" % (CHUNKS - 1))
        nc.tensor.transpose(g_ps[:], g_rows[:], ident[:])
        g_cols = tile([P, 2 * PACK], F32, "g_cols")
        nc.scalar.copy(out=g_cols[:], in_=g_ps[:, 0 : 2 * PACK])

        xv_s_raw = tile([P, H], U8, "xv_s_raw")
        xv_s = tile([P, H], U8, "xv_s")
        xq_s = tile([P, S], U8, "xq_s")
        dk_s_raw = tile([P, H], U8, "dk_s_raw")
        xv_w = tile([P, H], U32, "xv_w")
        dk_w = tile([P, H], U32, "dk_w")
        nc.vector.tensor_copy(xv_s_raw[:], xs_win[:].indirect(vidx_t[:]))
        nc.vector.tensor_copy(xq_s[:], xs_win[:].indirect(offs_t[:]))
        deal_scales(xv_s, xv_s_raw)
        nc.vector.tensor_copy(dealt(xv_w[:]), xw_win[:].indirect(vidx_t[:]))
        nc.vector.tensor_copy(dk_s_raw[:], ds_win[:].indirect(kidx_t[:]))
        quantise(wv_w[:, 0:HALF], wv_s[:, 0:HALF], wv_bf[0][:])
        dk_s = shared.tile([P, H], U8, name="dk_s", offset=0, align_bytes=64)
        deal_scales(dk_s, dk_s_raw)
        for j in range(4):
            nc.sync.dma_start(
                out=dk_plane[j:P:QUADRANT, :].bitcast(I32), in_=dk_s[BLOCK_PARTS * j : P : QUADRANT, :].bitcast(I32)
            )
        quantise(wv_w[:, HALF:N], wv_s[:, HALF:N], wv_bf[1][:])
        xq_w = shared.tile([P, S], U32, name="xq_w", offset=H, align_bytes=64)
        dk_w_raw = tile([P, H], U32, "dk_w_raw", tag="wv_bf1_bytes")
        nc.vector.tensor_copy(xq_w[:], xw_win[:].indirect(offs_t[:]))
        nc.vector.tensor_copy(dk_w_raw[:], dw_win[:].indirect(kidx_t[:]))
        nc.vector.tensor_copy(
            out=dealt(dk_w[:]), in_=dk_w_raw[:].rearrange("p (a t r) -> p a t r", t=PACK, r=BLOCK_PARTS)
        )

        z_tiles = tile([P, PACK, N], BF16, "z_tiles")
        z_by_half = z_tiles[:].rearrange("p t (u h f) -> p t h u f", u=PACK, h=2)
        for h in range(2):
            cols = slice(h * HALF, (h + 1) * HALF)
            for pair in range(2):
                val = ps.tile([P, 2, HALF], F32, name="val%d%d" % (h, pair), tag="value%d" % (2 * h + pair))
                for e in range(2):
                    keys = slice((2 * pair + e) * P, (2 * pair + e + 1) * P)
                    matmul(val[:, e, :], xv_w[:, keys], xv_s[:, keys], wv_w[:, cols], wv_s[:, cols])
                for e in range(2):
                    t = 2 * pair + e
                    nc.scalar.activation(
                        out=z_by_half[:, t, h], in_=val[:, e, :].rearrange("p (f u) -> p u f", u=PACK),
                        func=ACT.Copy, scale=g_cols[:, t : t + 1],
                    )
        z_bf = tile([P, N, PACK], BF16, "z_bf")
        z_w = tile([P, N], U32, "z_w")
        z_s = tile([P, N], U8, "z_s")
        dst, src = interleave_views(z_bf[:, 0:Z_ON_SCALAR, :], z_tiles[:, :, 0:Z_ON_SCALAR])
        nc.scalar.copy(out=dst, in_=src)
        dst, src = interleave_views(z_bf[:, Z_ON_SCALAR:N, :], z_tiles[:, :, Z_ON_SCALAR:N])
        nc.vector.tensor_copy(out=dst, in_=src)

        gt_b = g_cols[:, PACK : 2 * PACK].unsqueeze(1).to_broadcast([P, CHUNK, PACK])
        out_rows = out_0.rearrange("(p u) j -> p u j", u=PACK)
        y_w = tile([P, S], U32, "y_w")
        y_s = tile([P, S], U8, "y_s")
        th = [tile([P, CHUNK, PACK], F32, "th%d" % c) for c in range(CHUNKS)]
        z2_bf = [tile([P, CHUNK, PACK], BF16, "z2_bf%d" % c) for c in range(CHUNKS)]
        z2_w = [tile([P, CHUNK], U32, "z2_w%d" % c) for c in range(CHUNKS)]
        z2_s = [tile([P, CHUNK], U8, "z2_s%d" % c) for c in range(CHUNKS)]
        y = [tile([P, PACK, (hi - lo) * CHUNK], F32, "y%d" % lo) for lo, hi in SPANS]
        y_bf = [tile([P, (hi - lo) * CHUNK, PACK], BF16, "y_bf%d" % lo) for lo, hi in SPANS]
        span_of = [n for n, (lo, hi) in enumerate(SPANS) for c in range(lo, hi)]

        def scores(c):
            cols = slice(c * CHUNK, (c + 1) * CHUNK)
            s_ps = ps.tile([P, PACK, CHUNK], F32, name="s_ps%d" % c, tag="score%d" % c)
            for t in range(PACK):
                keys = slice(t * P, (t + 1) * P)
                matmul(s_ps[:, t, :], dk_w[:, keys], dk_plane[:, keys], xq_w[:, cols], xq_s[:, cols])
            nc.scalar.activation(out=th[c][:], in_=s_ps[:].rearrange("p t j -> p j t"), func=ACT.Tanh, scale=SIXTEENTH)

        def weigh(c):
            nc.vector.tensor_tensor(out=z2_bf[c][:], in0=th[c][:], in1=gt_b, op=MULT)

        def product(c):
            quantise(z2_w[c][:], z2_s[c][:], z2_bf[c][:])
            o_ps = ps.tile([P, PACK, CHUNK], F32, name="o_ps%d" % c, tag="value%d" % c)
            for u in range(PACK):
                feats = slice(u * P, (u + 1) * P)
                matmul(o_ps[:, u, :], z_w[:, feats], z_s[:, feats], z2_w[c][:], z2_s[c][:])
            span = span_of[c]
            first = (c - SPANS[span][0]) * CHUNK
            y_part = y[span][:, :, first : first + CHUNK]
            nc.scalar.activation(out=y_part, in_=o_ps[:], func=ACT.Copy, scale=SIXTEENTH)
            nc.sync.dma_start(out=out_rows[:, :, c * CHUNK : (c + 1) * CHUNK], in_=y_part)
            if c == CHUNKS - 1:
                nc.scalar.activation(
                    out=y_bf[span][:], in_=o_ps[:].rearrange("p u j -> p j u"), func=ACT.Copy, scale=SIXTEENTH
                )

        for c in range(CHUNKS):
            scores(c)
        weigh(0)
        quantise(z_w[:], z_s[:], z_bf[:])
        for c in range(CHUNKS):
            if c + 1 < CHUNKS:
                weigh(c + 1)
            product(c)

        for span in range(len(SPANS) - 1):
            dst, src = interleave_views(y_bf[span][:], y[span][:])
            nc.vector.tensor_copy(out=dst, in_=src)
        for span, (lo, hi) in enumerate(SPANS):
            cols = slice(lo * CHUNK, hi * CHUNK)
            quantise(y_w[:, cols], y_s[:, cols], y_bf[span][:])

        words_out = word_rows(out_1)
        last = S - CHUNK
        nc.sync.dma_start(out=words_out[:, 0:last], in_=y_w[:, 0:last].bitcast(I32))
        nc.sync.dma_start(out=words_out[:, last:S], in_=y_w[:, last:S].bitcast(I32))
        for q in range(P // QUADRANT):
            queue = nc.scalar if q % 2 else nc.sync
            queue.dma_start(
                out=out_2[0, 4 * q : 4 * q + 4, :].bitcast(I32),
                in_=y_s[QUADRANT * q : QUADRANT * q + 4, :].bitcast(I32),
            )
